import numpy as np
import ml_dtypes


def mxq(x, axis, fmt="e4m3"):
    dtype, down = {"e4m3": (ml_dtypes.float8_e4m3fn, 7), "e5m2": (ml_dtypes.float8_e5m2, 14)}[fmt]
    v = np.moveaxis(np.asarray(x, np.float32).astype(ml_dtypes.bfloat16).astype(np.float64), axis, -1)
    blocks = v.reshape(v.shape[:-1] + (-1, 32))
    amax = np.abs(blocks).max(-1, keepdims=True)
    byte = np.maximum(np.where(amax > 0, np.frexp(amax)[1] - 1 + 127, 0) - down, 1)
    scale = np.exp2(byte - 127.0)
    codes = (blocks / scale).astype(np.float32).astype(dtype).astype(np.float64)
    return np.moveaxis((codes * scale).reshape(v.shape), -1, axis)


WIDE = False


def mx_kscale(k):
    if not WIDE:
        return np.ones(k)
    levels = np.array([10, -10, 5, -5, 0])
    if k % 512:
        return np.exp2(np.random.permutation(np.resize(levels, k // 32))).repeat(32)
    a = np.empty((k // 512, 16))
    for p in range(k // 512):
        a[p, :8] = np.random.permutation(np.resize(levels, 8))
        for g in range(8):
            far = levels[np.abs(levels - a[p, g]) >= 10]
            a[p, g + 8] = far[np.random.randint(len(far))]
    return np.exp2(a.ravel()).repeat(32)


def f64(x):
    return np.asarray(x).astype(np.float64)


def striped(idx):
    return np.tile(idx.reshape(-1, 16).T, (8, 1)).astype(np.uint16)


def unstriped(offs):
    return offs[:16].T.reshape(-1).astype(np.int64)


def striped8(idx):
    return np.concatenate([x.reshape(-1, 16).T for x in idx]).astype(np.uint16)


def runs(offs, k):
    lists = np.stack([offs[16 * r : 16 * r + 16].T.reshape(-1) for r in range(8)]).astype(np.int64)
    return lists[np.arange(k) % 512 // 64]


def pack_weight(w):
    k, n = w.shape
    w = f64(np.asarray(w, np.float32).astype(ml_dtypes.bfloat16)).reshape(k // 32, 32, n)
    amax = np.abs(w).max(1)
    byte = np.clip(np.where(amax > 0, np.frexp(amax)[1] - 1 + 127 - 7, 1), 1, 254)
    scaled = (w * np.exp2(127.0 - byte)[:, None, :]).reshape(k, n).astype(np.float32)
    words = np.ascontiguousarray(scaled.reshape(k // 512, 128, 4, n).transpose(0, 1, 3, 2)).astype(ml_dtypes.float8_e4m3fn).view(np.uint8)
    return words, np.ascontiguousarray(byte.astype(np.uint8).reshape(k // 512, 16, n))


def unpack_weight(words, scales):
    g, p, n, _ = words.shape
    vals = np.ascontiguousarray(words).view(ml_dtypes.float8_e4m3fn).astype(np.float64) * np.repeat(np.exp2(scales.astype(np.float64) - 127.0), 8, axis=1)[..., None]
    return vals.transpose(0, 1, 3, 2).reshape(g * 512, n)

def planes(y):
    n, m = y.shape
    v = y.astype(np.float32).astype(ml_dtypes.bfloat16).astype(np.float64).reshape(n // 32, 32, m)
    top = np.abs(v).max(1)
    byte = np.clip(np.where(top > 0, np.frexp(top)[1] - 1 + 127 - 7, 1), 1, 254)
    codes = (v * np.exp2(127.0 - byte)[:, None, :]).reshape(n, m).astype(np.float32).astype(ml_dtypes.float8_e4m3fn).view(np.uint8)
    words = codes.reshape(n // 512, 128, 4, m).transpose(0, 1, 3, 2)
    return np.ascontiguousarray(words), np.ascontiguousarray(byte.astype(np.uint8).reshape(n // 512, 16, m))


K, T, S, V, H = 512, 2048, 512, 512, 512


def setup_inputs():
    n = np.random.standard_normal
    s = mx_kscale(K)[:, None]
    u = mx_kscale(S)
    packed_xT = pack_weight(n((K, T)) * s)
    packed_w1 = pack_weight(n((K, H)) / np.sqrt(K) / s)
    packed_w2 = pack_weight(n((K, H)) / np.sqrt(K) / s)
    packed_w3 = pack_weight(n((K, H)) / np.sqrt(K) / s)
    return {
        "x_words": packed_xT[0],
        "x_scales": packed_xT[1],
        "w1_words": packed_w1[0],
        "w1_scales": packed_w1[1],
        "w2_words": packed_w2[0],
        "w2_scales": packed_w2[1],
        "w3_words": packed_w3[0],
        "w3_scales": packed_w3[1],
        "ga": (np.random.uniform(0.5, 1.5, (H, 1)) * u[:, None]).astype(np.float32),
        "gb": (np.random.uniform(0.5, 1.5, (H, 1)) / u[:, None]).astype(np.float32),
        "offs": striped(np.random.permutation(T)[:S]),
        "two": striped(np.random.permutation(T)[:S]),
        "n1": striped8(np.stack([np.random.permutation(S) for _ in range(8)])),
        "n2": striped8(np.stack([np.random.permutation(S) for _ in range(8)])),
        "n3": striped8(np.stack([np.random.permutation(S) for _ in range(8)])),
        "n4": striped8(np.stack([np.random.permutation(S) for _ in range(8)])),
        "three": striped(np.random.permutation(T)[:V]),
        "n5": striped8(np.stack([np.random.permutation(V) for _ in range(8)])),
        "n6": striped8(np.stack([np.random.permutation(V) for _ in range(8)])),
        "n7": striped8(np.stack([np.random.permutation(V) for _ in range(8)])),
        "n8": striped8(np.stack([np.random.permutation(V) for _ in range(8)])),
        "n9": striped8(np.stack([np.random.permutation(V) for _ in range(8)])),
    }


def reference(x_words, x_scales, w1_words, w1_scales, w2_words, w2_scales, w3_words, w3_scales, ga, gb, offs, two, n1, n2, n3, n4, three, n5, n6, n7, n8, n9):
    xq = unpack_weight(x_words, x_scales)[:, unstriped(offs)]
    y = unpack_weight(w1_words, w1_scales).T @ xq
    x_two = unpack_weight(x_words, x_scales)[:, unstriped(two)]
    d = unpack_weight(w2_words, w2_scales).T @ x_two
    z = f64(ga) * (np.maximum(y[np.arange(H)[:, None], runs(n1, H)] + d[np.arange(H)[:, None], runs(n3, H)], y[np.arange(H)[:, None], runs(n2, H)] + d[np.arange(H)[:, None], runs(n4, H)]))
    x_three = unpack_weight(x_words, x_scales)[:, unstriped(three)]
    b = unpack_weight(w3_words, w3_scales).T @ x_three
    z2 = f64(gb) * (b * (b[np.arange(H)[:, None], runs(n5, H)] - (b[np.arange(H)[:, None], runs(n6, H)])))
    s = 0.0625 * ((mxq(z, 0, "e4m3").T @ mxq(z2, 0, "e4m3")))
    st = s - (s[np.arange(S)[:, None], runs(n7, S)])
    su = np.maximum(st, st[np.arange(S)[:, None], runs(n8, S)])
    out_0 = su + 0.5 * (su[np.arange(S)[:, None], runs(n9, S)])
    return (out_0,) + planes(out_0)

@@ -1,0 +1,242 @@
+from contextlib import ExitStack
+
+import concourse.mybir as mybir
+from concourse.masks import make_identity
+
+F32 = mybir.dt.float32
+BF16 = mybir.dt.bfloat16
+I32 = mybir.dt.int32
+U32 = mybir.dt.uint32
+U16 = mybir.dt.uint16
+U8 = mybir.dt.uint8
+FP8X4 = mybir.dt.float8_e4m3fn_x4
+ALU = mybir.AluOpType
+ACT = mybir.ActivationFunctionType
+
+P = 128
+PACK = 4
+T = 2048
+N = 512
+HALF = N // 2
+OUT_SLICES = ((0, 256), (256, 384), (384, 512))
+FLOPS = 4 * 2 * 512 * 512 * 512
+
+
+def tile_picked_twkpathbwindthree_none_po_kernel(
+    tc, x_words, x_scales, w1_words, w1_scales, w2_words, w2_scales, w3_words, w3_scales, ga, gb,
+    offs, two, n1, n2, n3, n4, three, n5, n6, n7, n8, n9, out_0, out_1, out_2,
+):
+    nc = tc.nc
+    with ExitStack() as ctx:
+        lists = ctx.enter_context(tc.tile_pool(name="lists", bufs=1))
+        keep = ctx.enter_context(tc.tile_pool(name="keep", bufs=1))
+        psum = ctx.enter_context(tc.psum_pool(name="psum", bufs=8))
+
+        def sb(name, shape, dtype):
+            return keep.tile(shape, dtype, name=name, align_bytes=64)
+
+        def bank():
+            return psum.tile([P, N], F32, name="bank")
+
+        def load_list(name, dram):
+            tile = lists.tile([P, N // 16], U16, name=name)
+            nc.sync.dma_start(tile[:], dram)
+            return tile
+
+        def load_scales(queue, tile, first, dram):
+            for q in range(4):
+                queue.dma_start(tile[32 * q + first : 32 * q + first + 4, :].bitcast(I32), dram[0][4 * q : 4 * q + 4, :].bitcast(I32))
+
+        def load_words(name, dram, width):
+            tile = sb(name, [P, width], I32)
+            nc.sync.dma_start(tile[:], dram[0].rearrange("p n t -> p (n t)").bitcast(I32))
+            return tile
+
+        def entries(tile, lo, hi):
+            return tile[:, lo // 16 : hi // 16]
+
+        xs = sb("xs", [P, T], U8)
+        ws = sb("ws", [P, N], U8)
+        nc.vector.memset(xs[:].bitcast(I32), 0)
+        nc.vector.memset(ws[:].bitcast(I32), 0)
+        win_a = [sb("win_a%d" % t, [P, 2 * N], F32) for t in range(PACK)]
+        win_d = [sb("win_d%d" % t, [P, 2 * N], F32) for t in range(PACK)]
+        for tile in win_a + win_d:
+            nc.vector.memset(tile[:, N:], 0.0)
+
+        l_offs = load_list("l_offs", offs)
+        l_two = load_list("l_two", two)
+        load_scales(nc.sync, xs, 0, x_scales)
+        xw = load_words("xw", x_words, T)
+        w1r = load_words("w1r", w1_words, N)
+        load_scales(nc.gpsimd, ws, 8, w3_scales)
+        load_scales(nc.sync, ws, 0, w1_scales)
+        load_scales(nc.sync, ws, 4, w2_scales)
+        w2r = load_words("w2r", w2_words, N)
+        l_three = load_list("l_three", three)
+        ga_sb = sb("ga_sb", [P, PACK], F32)
+        gb_sb = sb("gb_sb", [P, PACK], F32)
+        nc.gpsimd.dma_start(ga_sb[:], ga.rearrange("(p t) o -> p (t o)", t=PACK))
+        nc.gpsimd.dma_start(gb_sb[:], gb.rearrange("(p t) o -> p (t o)", t=PACK))
+        l1 = load_list("l1", n1)
+        l3 = load_list("l3", n3)
+        l2 = load_list("l2", n2)
+        l4 = load_list("l4", n4)
+        w3r = load_words("w3r", w3_words, N)
+        l5 = load_list("l5", n5)
+        l6 = load_list("l6", n6)
+        l7 = load_list("l7", n7)
+        l8 = load_list("l8", n8)
+        l9 = load_list("l9", n9)
+
+        ident = sb("ident", [P, P], F32)
+        make_identity(nc, ident[:])
+
+        ga_abs = sb("ga_abs", [P, PACK], F32)
+        ga_negsign = sb("ga_negsign", [P, PACK], F32)
+        gb_neg = sb("gb_neg", [P, PACK], F32)
+        nc.scalar.activation(ga_abs[:], ga_sb[:], ACT.Abs)
+        nc.scalar.activation(ga_negsign[:], ga_sb[:], ACT.Sign, scale=-1.0)
+        nc.gpsimd.tensor_tensor(gb_neg[:], ga_negsign[:], gb_sb[:], ALU.mult)
+
+        def gather_scales(name, lst):
+            tile = sb(name, [P, N], U8)
+            nc.vector.tensor_copy(tile[:], xs[:].indirect(lst[:]))
+            return tile
+
+        def gather_words(name, lst):
+            tile = sb(name, [P, N], U32)
+            nc.vector.tensor_copy(tile[:], xw[:].bitcast(U32).indirect(lst[:]))
+            return tile
+
+        def deal(name, raw, dtype):
+            tile = sb(name, [P, N], dtype)
+            nc.vector.tensor_copy(tile[:].rearrange("p (t m) -> p m t", t=PACK), raw[:].rearrange("p (m t) -> p m t", t=PACK))
+            return tile
+
+        def project(w, first, xg, xsg, t):
+            acc = bank()
+            cols = slice(t * P, (t + 1) * P)
+            nc.tensor.matmul_mx(acc[:], lhsT=w[:, cols].bitcast(FP8X4), lhsT_scale=wsd[first:P, cols],
+                                rhs=xg[:].bitcast(FP8X4), rhs_scale=xsg[:], start=True, stop=True)
+            return acc
+
+        xs1 = gather_scales("xs1", l_offs)
+        xs2 = gather_scales("xs2", l_two)
+        xg1 = gather_words("xg1", l_offs)
+        w1 = deal("w1", w1r, I32)
+        xg2 = gather_words("xg2", l_two)
+        wsd = deal("wsd", ws, U8)
+        w2 = deal("w2", w2r, I32)
+        for t in range(PACK):
+            nc.scalar.activation(win_a[t][:, :N], project(w1, 0, xg1, xs1, t)[:], ACT.Copy, scale=ga_abs[:, t : t + 1])
+            nc.scalar.activation(win_d[t][:, :N], project(w2, 4, xg2, xs2, t)[:], ACT.Copy, scale=ga_abs[:, t : t + 1])
+        xs3 = gather_scales("xs3", l_three)
+        xg3 = gather_words("xg3", l_three)
+        w3 = deal("w3", w3r, I32)
+        win_b = [sb("win_b%d" % t, [P, N], F32) for t in range(PACK)]
+        nbg = sb("nbg", [P, PACK, N], F32)
+        for t in range(PACK):
+            acc = project(w3, 8, xg3, xs3, t)
+            nc.scalar.copy(win_b[t][:], acc[:])
+            nc.scalar.activation(nbg[:, t, :], acc[:], ACT.Copy, scale=gb_neg[:, t : t + 1])
+
+        first_y = [sb("first_y%d" % t, [P, N], F32) for t in range(PACK)]
+        first_sum = [sb("first_sum%d" % t, [P, N], F32) for t in range(PACK)]
+        part = [sb("part%d" % t, [P, N], F32) for t in range(PACK)]
+        gap = [sb("gap%d" % t, [P, N], F32) for t in range(PACK)]
+        rise = [sb("rise%d" % t, [P, N], F32) for t in range(PACK)]
+        for pair in ((0, 1), (2, 3)):
+            for t in pair:
+                nc.vector.tensor_copy(first_y[t][:], win_a[t][:].indirect(l1[:]))
+            for t in pair:
+                nc.vector.tensor_tensor(first_sum[t][:], win_d[t][:].indirect(l3[:]), first_y[t][:], ALU.add)
+            for t in pair:
+                nc.vector.tensor_tensor(part[t][:], win_a[t][:].indirect(l2[:]), first_sum[t][:], ALU.subtract)
+            for t in pair:
+                nc.vector.tensor_tensor(gap[t][:], win_d[t][:].indirect(l4[:]), part[t][:], ALU.add)
+                nc.scalar.activation(rise[t][:], gap[t][:], ACT.Relu)
+        z_turned = [bank() for jb in range(4)]
+        for t in range(PACK):
+            for jb in range(4):
+                cols = slice(jb * P, (jb + 1) * P)
+                dst = z_turned[jb][:, t * P : (t + 1) * P]
+                nc.tensor.matmul(dst, first_sum[t][:, cols], ident[:], start=True, stop=False, is_transpose=True)
+                nc.tensor.matmul(dst, rise[t][:, cols], ident[:], start=False, stop=True, is_transpose=True)
+        z_rows = [sb("z_rows%d" % jb, [P, N], BF16) for jb in range(4)]
+        for jb in range(4):
+            nc.scalar.copy(z_rows[jb][:].rearrange("c (u p e) -> c u p e", u=2, e=2), z_turned[jb][:].rearrange("c (u e p) -> c u p e", u=2, e=2))
+        zb = sb("zb", [P, N * PACK], BF16)
+        for jh in range(2):
+            back = bank()
+            for u in range(2):
+                for jl in range(2):
+                    nc.tensor.transpose(back[:, u * 256 + jl * P : u * 256 + (jl + 1) * P], z_rows[2 * jh + jl][:].bitcast(F32)[:, u * P : (u + 1) * P], ident[:])
+            nc.scalar.copy(
+                zb[:].bitcast(F32).rearrange("p (r h m u) -> p r h m u", r=4, h=2, u=2)[:, :, jh],
+                back[:].rearrange("p (u m r) -> p r m u", u=2, r=4),
+            )
+        zq = sb("zq", [P, N], U32)
+        zs = sb("zs", [P, N], U8)
+        nc.vector.quantize_mx(zq[:].bitcast(FP8X4), zs[:], zb[:])
+
+        s_banks = [bank() for r in range(PACK)]
+        s_plain = [sb("s_plain%d" % r, [P, N], F32) for r in range(PACK)]
+        for h in range(2):
+            lo, hi = h * HALF, (h + 1) * HALF
+            at5 = sb("at5_%d" % h, [P, PACK, HALF], F32)
+            ndiff = sb("ndiff%d" % h, [P, PACK, HALF], F32)
+            for t in range(PACK):
+                nc.vector.tensor_copy(at5[:, t, :], win_b[t][:].indirect(entries(l5, lo, hi)))
+            for t in range(PACK):
+                nc.vector.tensor_tensor(ndiff[:, t, :], win_b[t][:].indirect(entries(l6, lo, hi)), at5[:, t, :], ALU.subtract)
+            z2b = sb("z2b%d" % h, [P, HALF * PACK], BF16)
+            nc.vector.tensor_tensor(
+                z2b[:].rearrange("p (c i t) -> p c t i", i=4, t=PACK),
+                ndiff[:].rearrange("p t (c i) -> p c t i", i=4),
+                nbg[:, :, lo:hi].rearrange("p t (c i) -> p c t i", i=4),
+                ALU.mult,
+            )
+            z2q = sb("z2q%d" % h, [P, HALF], U32)
+            z2s = sb("z2s%d" % h, [P, HALF], U8)
+            nc.vector.quantize_mx(z2q[:].bitcast(FP8X4), z2s[:], z2b[:])
+            for r in range(PACK):
+                cols = slice(r * P, (r + 1) * P)
+                nc.tensor.matmul_mx(s_banks[r][:, lo:hi], lhsT=zq[:, cols].bitcast(FP8X4), lhsT_scale=zs[:, cols],
+                                    rhs=z2q[:].bitcast(FP8X4), rhs_scale=z2s[:], start=True, stop=True)
+                nc.scalar.activation(win_a[r][:, lo:hi], s_banks[r][:, lo:hi], ACT.Copy, scale=-0.0625)
+                nc.scalar.activation(s_plain[r][:, lo:hi], s_banks[r][:, lo:hi], ACT.Copy, scale=0.0625)
+
+        at8 = [sb("at8_%d" % r, [P, N], F32) for r in range(PACK)]
+        su = [sb("su%d" % r, [P, N], F32) for r in range(PACK)]
+        half_su = [sb("half_su%d" % r, [P, N], F32) for r in range(PACK)]
+        for r in range(PACK):
+            nc.vector.tensor_tensor(win_d[r][:, :N], win_a[r][:].indirect(l7[:]), s_plain[r][:], ALU.add)
+        for r in range(PACK + 1):
+            if r < PACK:
+                nc.vector.tensor_copy(at8[r][:], win_d[r][:].indirect(l8[:]))
+            if r > 0:
+                nc.vector.tensor_tensor(su[r - 1][:], win_d[r - 1][:, :N], at8[r - 1][:], ALU.max)
+                nc.scalar.activation(half_su[r - 1][:], su[r - 1][:], ACT.Copy, scale=0.5)
+        out_rows = out_0.rearrange("(p r) v -> p r v", r=PACK)
+        out_words = out_1[0].rearrange("p c r -> p (c r)").bitcast(I32)
+        os_ = sb("os", [P, N], U8)
+        for i, (lo, hi) in enumerate(OUT_SLICES):
+            width = hi - lo
+            res = sb("res%d" % i, [P, PACK, width], F32)
+            for r in range(PACK):
+                nc.vector.tensor_tensor(res[:, r, :], half_su[r][:].indirect(entries(l9, lo, hi)), su[r][:, lo:hi], ALU.add)
+            nc.sync.dma_start(out_rows[:, :, lo:hi], res[:])
+            ob = sb("ob%d" % i, [P, width * PACK], BF16)
+            weave_out = ob[:].rearrange("p (c i r) -> p c r i", i=4, r=PACK)
+            weave_in = res[:].rearrange("p r (c i) -> p c r i", i=4)
+            if hi < N:
+                nc.scalar.copy(weave_out, weave_in)
+            else:
+                nc.vector.tensor_copy(weave_out, weave_in)
+            oq = sb("oq%d" % i, [P, width], I32)
+            nc.vector.quantize_mx(oq[:].bitcast(FP8X4), os_[:, lo:hi], ob[:])
+            nc.scalar.dma_start(out_words[:, lo:hi], oq[:])
+        for q in range(4):
+            queue = nc.sync if q % 2 == 0 else nc.scalar
+            queue.dma_start(out_2[0][4 * q : 4 * q + 4, :].bitcast(I32), os_[32 * q : 32 * q + 4, :].bitcast(I32))

@@ -43,48 +43,52 @@ def tile_picked_twkpathbwindthree_none_po_kernel(
             nc.sync.dma_start(tile[:], dram)
             return tile
 
-        def load_scales(queue, tile, first, dram):
+        def load_scales(plane, dram):
             for q in range(4):
-                queue.dma_start(tile[32 * q + first : 32 * q + first + 4, :].bitcast(I32), dram[0][4 * q : 4 * q + 4, :].bitcast(I32))
+                nc.sync.dma_start(plane[32 * q : 32 * q + 4, :].bitcast(I32), dram[0][4 * q : 4 * q + 4, :].bitcast(I32))
 
         def load_words(name, dram, width):
             tile = sb(name, [P, width], I32)
             nc.sync.dma_start(tile[:], dram[0].rearrange("p n t -> p (n t)").bitcast(I32))
             return tile
 
+        def load_gain(rows, dram):
+            nc.sync.dma_start(rows.rearrange("t (g r) -> t g r", r=8), dram.rearrange("(g t r) o -> t g (r o)", t=PACK, r=8))
+
         def entries(tile, lo, hi):
             return tile[:, lo // 16 : hi // 16]
 
         xs = sb("xs", [P, T], U8)
-        ws = sb("ws", [P, N], U8)
+        ws = sb("ws", [P, 3 * N], U8)
+        gain_rows = sb("gain_rows", [P, P], F32)
         nc.vector.memset(xs[:].bitcast(I32), 0)
+        nc.vector.memset(gain_rows[:], 0.0)
         nc.vector.memset(ws[:].bitcast(I32), 0)
         win_a = [sb("win_a%d" % t, [P, 2 * N], F32) for t in range(PACK)]
         win_d = [sb("win_d%d" % t, [P, 2 * N], F32) for t in range(PACK)]
-        for tile in win_a + win_d:
-            nc.vector.memset(tile[:, N:], 0.0)
+        win_b = [sb("win_b%d" % t, [P, 2 * N], F32) for t in range(PACK)]
+        for t in range(PACK):
+            nc.vector.memset(win_b[t][:, N:], 0.0)
 
+        l_three = load_list("l_three", three)
         l_offs = load_list("l_offs", offs)
         l_two = load_list("l_two", two)
-        load_scales(nc.sync, xs, 0, x_scales)
+        load_scales(xs[:], x_scales)
         xw = load_words("xw", x_words, T)
+        load_gain(gain_rows[0:PACK, :], ga)
+        load_gain(gain_rows[PACK : 2 * PACK, :], gb)
+        load_scales(ws[:, 2 * N :], w3_scales)
+        w3r = load_words("w3r", w3_words, N)
+        l5 = load_list("l5", n5)
+        l6 = load_list("l6", n6)
+        load_scales(ws[:, :N], w1_scales)
+        load_scales(ws[:, N : 2 * N], w2_scales)
         w1r = load_words("w1r", w1_words, N)
-        load_scales(nc.gpsimd, ws, 8, w3_scales)
-        load_scales(nc.sync, ws, 0, w1_scales)
-        load_scales(nc.sync, ws, 4, w2_scales)
         w2r = load_words("w2r", w2_words, N)
-        l_three = load_list("l_three", three)
-        ga_sb = sb("ga_sb", [P, PACK], F32)
-        gb_sb = sb("gb_sb", [P, PACK], F32)
-        nc.gpsimd.dma_start(ga_sb[:], ga.rearrange("(p t) o -> p (t o)", t=PACK))
-        nc.gpsimd.dma_start(gb_sb[:], gb.rearrange("(p t) o -> p (t o)", t=PACK))
         l1 = load_list("l1", n1)
         l3 = load_list("l3", n3)
         l2 = load_list("l2", n2)
         l4 = load_list("l4", n4)
-        w3r = load_words("w3r", w3_words, N)
-        l5 = load_list("l5", n5)
-        l6 = load_list("l6", n6)
         l7 = load_list("l7", n7)
         l8 = load_list("l8", n8)
         l9 = load_list("l9", n9)
@@ -95,9 +99,14 @@ def tile_picked_twkpathbwindthree_none_po_kernel(
         ga_abs = sb("ga_abs", [P, PACK], F32)
         ga_negsign = sb("ga_negsign", [P, PACK], F32)
         gb_neg = sb("gb_neg", [P, PACK], F32)
-        nc.scalar.activation(ga_abs[:], ga_sb[:], ACT.Abs)
-        nc.scalar.activation(ga_negsign[:], ga_sb[:], ACT.Sign, scale=-1.0)
-        nc.gpsimd.tensor_tensor(gb_neg[:], ga_negsign[:], gb_sb[:], ALU.mult)
+        gains = bank()
+        nc.tensor.transpose(gains[:, :P], gain_rows[:], ident[:])
+        nc.scalar.activation(ga_abs[:], gains[:, 0:PACK], ACT.Abs)
+        nc.scalar.activation(ga_negsign[:], gains[:, 0:PACK], ACT.Sign, scale=-1.0)
+        for t in range(PACK):
+            nc.scalar.activation(gb_neg[:, t : t + 1], gains[:, PACK + t : PACK + t + 1], ACT.Copy, scale=ga_negsign[:, t : t + 1])
+        gb_pos = sb("gb_pos", [P, PACK], F32)
+        nc.scalar.activation(gb_pos[:], gb_neg[:], ACT.Copy, scale=-1.0)
 
         def gather_scales(name, lst):
             tile = sb(name, [P, N], U8)
@@ -109,103 +118,101 @@ def tile_picked_twkpathbwindthree_none_po_kernel(
             nc.vector.tensor_copy(tile[:], xw[:].bitcast(U32).indirect(lst[:]))
             return tile
 
-        def deal(name, raw, dtype):
-            tile = sb(name, [P, N], dtype)
-            nc.vector.tensor_copy(tile[:].rearrange("p (t m) -> p m t", t=PACK), raw[:].rearrange("p (m t) -> p m t", t=PACK))
+        def deal(name, raw, dtype, tag):
+            tile = keep.tile([P, N], dtype, name=name, tag=tag, align_bytes=64)
+            nc.vector.tensor_copy(
+                tile[:].bitcast(I32).rearrange("p (t g r) -> p g t r", t=PACK, g=16),
+                raw.bitcast(I32).rearrange("p (g t r) -> p g t r", t=PACK, g=16),
+            )
             return tile
 
-        def project(w, first, xg, xsg, t):
+        def project(w, wscale, xg, xsg, t):
             acc = bank()
             cols = slice(t * P, (t + 1) * P)
-            nc.tensor.matmul_mx(acc[:], lhsT=w[:, cols].bitcast(FP8X4), lhsT_scale=wsd[first:P, cols],
+            nc.tensor.matmul_mx(acc[:], lhsT=w[:, cols].bitcast(FP8X4), lhsT_scale=wscale[:, cols],
                                 rhs=xg[:].bitcast(FP8X4), rhs_scale=xsg[:], start=True, stop=True)
             return acc
 
+        xs3 = gather_scales("xs3", l_three)
         xs1 = gather_scales("xs1", l_offs)
         xs2 = gather_scales("xs2", l_two)
-        xg1 = gather_words("xg1", l_offs)
-        w1 = deal("w1", w1r, I32)
-        xg2 = gather_words("xg2", l_two)
-        wsd = deal("wsd", ws, U8)
-        w2 = deal("w2", w2r, I32)
-        for t in range(PACK):
-            nc.scalar.activation(win_a[t][:, :N], project(w1, 0, xg1, xs1, t)[:], ACT.Copy, scale=ga_abs[:, t : t + 1])
-            nc.scalar.activation(win_d[t][:, :N], project(w2, 4, xg2, xs2, t)[:], ACT.Copy, scale=ga_abs[:, t : t + 1])
-        xs3 = gather_scales("xs3", l_three)
         xg3 = gather_words("xg3", l_three)
-        w3 = deal("w3", w3r, I32)
-        win_b = [sb("win_b%d" % t, [P, N], F32) for t in range(PACK)]
-        nbg = sb("nbg", [P, PACK, N], F32)
+        w3 = deal("w3", w3r[:], I32, "w13")
+        ws3 = deal("ws3", ws[:, 2 * N :], U8, "ws13")
+        bg = [sb("bg%d" % t, [P, N], F32) for t in range(PACK)]
+        nbg = [sb("nbg%d" % t, [P, N], F32) for t in range(PACK)]
         for t in range(PACK):
-            acc = project(w3, 8, xg3, xs3, t)
-            nc.scalar.copy(win_b[t][:], acc[:])
-            nc.scalar.activation(nbg[:, t, :], acc[:], ACT.Copy, scale=gb_neg[:, t : t + 1])
+            acc = project(w3, ws3, xg3, xs3, t)
+            nc.scalar.copy(win_b[t][:, :N], acc[:])
+            nc.scalar.activation(bg[t][:], acc[:], ACT.Copy, scale=gb_pos[:, t : t + 1])
+            nc.scalar.activation(nbg[t][:], acc[:], ACT.Copy, scale=gb_neg[:, t : t + 1])
+        xg1 = gather_words("xg1", l_offs)
+        xg2 = gather_words("xg2", l_two)
 
-        first_y = [sb("first_y%d" % t, [P, N], F32) for t in range(PACK)]
-        first_sum = [sb("first_sum%d" % t, [P, N], F32) for t in range(PACK)]
-        part = [sb("part%d" % t, [P, N], F32) for t in range(PACK)]
-        gap = [sb("gap%d" % t, [P, N], F32) for t in range(PACK)]
-        rise = [sb("rise%d" % t, [P, N], F32) for t in range(PACK)]
-        for pair in ((0, 1), (2, 3)):
-            for t in pair:
-                nc.vector.tensor_copy(first_y[t][:], win_a[t][:].indirect(l1[:]))
-            for t in pair:
-                nc.vector.tensor_tensor(first_sum[t][:], win_d[t][:].indirect(l3[:]), first_y[t][:], ALU.add)
-            for t in pair:
-                nc.vector.tensor_tensor(part[t][:], win_a[t][:].indirect(l2[:]), first_sum[t][:], ALU.subtract)
-            for t in pair:
-                nc.vector.tensor_tensor(gap[t][:], win_d[t][:].indirect(l4[:]), part[t][:], ALU.add)
-                nc.scalar.activation(rise[t][:], gap[t][:], ACT.Relu)
-        z_turned = [bank() for jb in range(4)]
+        turned = [bank() for jb in range(4)]
         for t in range(PACK):
+            plus = win_a[t][:, N:]
+            minus = win_d[t][:, N:]
+            nc.vector.tensor_tensor(plus, win_b[t][:].indirect(l5[:]), bg[t][:], ALU.mult)
+            nc.vector.tensor_tensor(minus, win_b[t][:].indirect(l6[:]), nbg[t][:], ALU.mult)
+            if t == 0:
+                w1 = deal("w1", w1r[:], I32, "w13")
+                ws1 = deal("ws1", ws[:, :N], U8, "ws13")
+                w2 = deal("w2", w2r[:], I32, "w2")
+                ws2 = deal("ws2", ws[:, N : 2 * N], U8, "ws2")
+            nc.scalar.activation(win_a[t][:, :N], project(w1, ws1, xg1, xs1, t)[:], ACT.Copy, scale=ga_abs[:, t : t + 1])
+            nc.scalar.activation(win_d[t][:, :N], project(w2, ws2, xg2, xs2, t)[:], ACT.Copy, scale=ga_abs[:, t : t + 1])
             for jb in range(4):
                 cols = slice(jb * P, (jb + 1) * P)
-                dst = z_turned[jb][:, t * P : (t + 1) * P]
-                nc.tensor.matmul(dst, first_sum[t][:, cols], ident[:], start=True, stop=False, is_transpose=True)
-                nc.tensor.matmul(dst, rise[t][:, cols], ident[:], start=False, stop=True, is_transpose=True)
-        z_rows = [sb("z_rows%d" % jb, [P, N], BF16) for jb in range(4)]
-        for jb in range(4):
-            nc.scalar.copy(z_rows[jb][:].rearrange("c (u p e) -> c u p e", u=2, e=2), z_turned[jb][:].rearrange("c (u e p) -> c u p e", u=2, e=2))
-        zb = sb("zb", [P, N * PACK], BF16)
+                dst = turned[jb][:, t * P : (t + 1) * P]
+                nc.tensor.matmul(dst, plus[:, cols], ident[:], start=True, stop=False, is_transpose=True)
+                nc.tensor.matmul(dst, minus[:, cols], ident[:], start=False, stop=True, is_transpose=True)
+        z2b = sb("z2b", [P, N * PACK], BF16)
         for jh in range(2):
             back = bank()
-            for u in range(2):
-                for jl in range(2):
-                    nc.tensor.transpose(back[:, u * 256 + jl * P : u * 256 + (jl + 1) * P], z_rows[2 * jh + jl][:].bitcast(F32)[:, u * P : (u + 1) * P], ident[:])
+            for jl in range(2):
+                jb = 2 * jh + jl
+                rows = sb("z2_rows%d" % jb, [P, N], BF16)
+                nc.scalar.copy(rows[:].rearrange("c (u p e) -> c u p e", u=2, e=2), turned[jb][:].rearrange("c (u e p) -> c u p e", u=2, e=2))
+                for u in range(2):
+                    nc.tensor.transpose(back[:, u * HALF + jl * P : u * HALF + (jl + 1) * P], rows[:].bitcast(F32)[:, u * P : (u + 1) * P], ident[:])
             nc.scalar.copy(
-                zb[:].bitcast(F32).rearrange("p (r h m u) -> p r h m u", r=4, h=2, u=2)[:, :, jh],
-                back[:].rearrange("p (u m r) -> p r m u", u=2, r=4),
+                z2b[:].bitcast(F32)[:, jh * N : (jh + 1) * N].rearrange("p (v u) -> p v u", u=2),
+                back[:].rearrange("p (u v) -> p v u", u=2),
             )
+        z2q = sb("z2q", [P, N], U32)
+        z2s = sb("z2s", [P, N], U8)
+        nc.vector.quantize_mx(z2q[:].bitcast(FP8X4), z2s[:], z2b[:])
+
+        first = sb("first", [P, PACK, N], F32)
+        second = sb("second", [P, PACK, N], F32)
+        for t in range(PACK):
+            y1 = sb("y1_%d" % t, [P, N], F32)
+            y2 = sb("y2_%d" % t, [P, N], F32)
+            nc.vector.tensor_copy(y1[:], win_a[t][:].indirect(l1[:]))
+            nc.vector.tensor_copy(y2[:], win_a[t][:].indirect(l2[:]))
+            nc.vector.tensor_tensor(first[:, t, :], win_d[t][:].indirect(l3[:]), y1[:], ALU.add)
+            nc.vector.tensor_tensor(second[:, t, :], win_d[t][:].indirect(l4[:]), y2[:], ALU.add)
         zq = sb("zq", [P, N], U32)
         zs = sb("zs", [P, N], U8)
-        nc.vector.quantize_mx(zq[:].bitcast(FP8X4), zs[:], zb[:])
-
-        s_banks = [bank() for r in range(PACK)]
         s_plain = [sb("s_plain%d" % r, [P, N], F32) for r in range(PACK)]
         for h in range(2):
-            lo, hi = h * HALF, (h + 1) * HALF
-            at5 = sb("at5_%d" % h, [P, PACK, HALF], F32)
-            ndiff = sb("ndiff%d" % h, [P, PACK, HALF], F32)
-            for t in range(PACK):
-                nc.vector.tensor_copy(at5[:, t, :], win_b[t][:].indirect(entries(l5, lo, hi)))
-            for t in range(PACK):
-                nc.vector.tensor_tensor(ndiff[:, t, :], win_b[t][:].indirect(entries(l6, lo, hi)), at5[:, t, :], ALU.subtract)
-            z2b = sb("z2b%d" % h, [P, HALF * PACK], BF16)
+            zb = sb("zb", [P, HALF * PACK], BF16)
             nc.vector.tensor_tensor(
-                z2b[:].rearrange("p (c i t) -> p c t i", i=4, t=PACK),
-                ndiff[:].rearrange("p t (c i) -> p c t i", i=4),
-                nbg[:, :, lo:hi].rearrange("p t (c i) -> p c t i", i=4),
-                ALU.mult,
+                zb[:].rearrange("p (r m t) -> p m t r", r=2, t=PACK),
+                first[:].rearrange("p t (m r) -> p m t r", r=PACK)[:, :, :, 2 * h : 2 * h + 2],
+                second[:].rearrange("p t (m r) -> p m t r", r=PACK)[:, :, :, 2 * h : 2 * h + 2],
+                ALU.max,
             )
-            z2q = sb("z2q%d" % h, [P, HALF], U32)
-            z2s = sb("z2s%d" % h, [P, HALF], U8)
-            nc.vector.quantize_mx(z2q[:].bitcast(FP8X4), z2s[:], z2b[:])
-            for r in range(PACK):
-                cols = slice(r * P, (r + 1) * P)
-                nc.tensor.matmul_mx(s_banks[r][:, lo:hi], lhsT=zq[:, cols].bitcast(FP8X4), lhsT_scale=zs[:, cols],
-                                    rhs=z2q[:].bitcast(FP8X4), rhs_scale=z2s[:], start=True, stop=True)
-                nc.scalar.activation(win_a[r][:, lo:hi], s_banks[r][:, lo:hi], ACT.Copy, scale=-0.0625)
-                nc.scalar.activation(s_plain[r][:, lo:hi], s_banks[r][:, lo:hi], ACT.Copy, scale=0.0625)
+            cols = slice(h * HALF, (h + 1) * HALF)
+            nc.vector.quantize_mx(zq[:, cols].bitcast(FP8X4), zs[:, cols], zb[:])
+        for r in range(PACK):
+            cols = slice(r * P, (r + 1) * P)
+            acc = bank()
+            nc.tensor.matmul_mx(acc[:], lhsT=zq[:, cols].bitcast(FP8X4), lhsT_scale=zs[:, cols],
+                                rhs=z2q[:].bitcast(FP8X4), rhs_scale=z2s[:], start=True, stop=True)
+            nc.scalar.activation(win_a[r][:, :N], acc[:], ACT.Copy, scale=-0.0625)
+            nc.scalar.activation(s_plain[r][:], acc[:], ACT.Copy, scale=0.0625)
 
         at8 = [sb("at8_%d" % r, [P, N], F32) for r in range(PACK)]
         su = [sb("su%d" % r, [P, N], F32) for r in range(PACK)]

@@ -48,7 +48,7 @@ def tile_picked_twkpathbwindthree_none_po_kernel(
                 nc.sync.dma_start(plane[32 * q : 32 * q + 4, :].bitcast(I32), dram[0][4 * q : 4 * q + 4, :].bitcast(I32))
 
         def load_words(name, dram, width):
-            tile = sb(name, [P, width], I32)
+            tile = keep.tile([P, width], I32, name=name, tag=name, align_bytes=64)
             nc.sync.dma_start(tile[:], dram[0].rearrange("p n t -> p (n t)").bitcast(I32))
             return tile
 
@@ -59,11 +59,12 @@ def tile_picked_twkpathbwindthree_none_po_kernel(
             return tile[:, lo // 16 : hi // 16]
 
         xs = sb("xs", [P, T], U8)
-        ws = sb("ws", [P, 3 * N], U8)
+        ws = [keep.tile([P, N], U8, name="ws_raw%d" % i, tag="ws_raw%d" % i, align_bytes=64) for i in range(3)]
         gain_rows = sb("gain_rows", [P, P], F32)
         nc.vector.memset(xs[:].bitcast(I32), 0)
         nc.vector.memset(gain_rows[:], 0.0)
-        nc.vector.memset(ws[:].bitcast(I32), 0)
+        for plane in reversed(ws):
+            nc.vector.memset(plane[:].bitcast(I32), 0)
         win_a = [sb("win_a%d" % t, [P, 2 * N], F32) for t in range(PACK)]
         win_d = [sb("win_d%d" % t, [P, 2 * N], F32) for t in range(PACK)]
         win_b = [sb("win_b%d" % t, [P, 2 * N], F32) for t in range(PACK)]
@@ -77,12 +78,12 @@ def tile_picked_twkpathbwindthree_none_po_kernel(
         xw = load_words("xw", x_words, T)
         load_gain(gain_rows[0:PACK, :], ga)
         load_gain(gain_rows[PACK : 2 * PACK, :], gb)
-        load_scales(ws[:, 2 * N :], w3_scales)
+        load_scales(ws[2][:], w3_scales)
         w3r = load_words("w3r", w3_words, N)
         l5 = load_list("l5", n5)
         l6 = load_list("l6", n6)
-        load_scales(ws[:, :N], w1_scales)
-        load_scales(ws[:, N : 2 * N], w2_scales)
+        load_scales(ws[0][:], w1_scales)
+        load_scales(ws[1][:], w2_scales)
         w1r = load_words("w1r", w1_words, N)
         w2r = load_words("w2r", w2_words, N)
         l1 = load_list("l1", n1)
@@ -113,8 +114,8 @@ def tile_picked_twkpathbwindthree_none_po_kernel(
             nc.vector.tensor_copy(tile[:], xs[:].indirect(lst[:]))
             return tile
 
-        def gather_words(name, lst):
-            tile = sb(name, [P, N], U32)
+        def gather_words(name, lst, tag):
+            tile = keep.tile([P, N], U32, name=name, tag=tag, align_bytes=64)
             nc.vector.tensor_copy(tile[:], xw[:].bitcast(U32).indirect(lst[:]))
             return tile
 
@@ -136,9 +137,9 @@ def tile_picked_twkpathbwindthree_none_po_kernel(
         xs3 = gather_scales("xs3", l_three)
         xs1 = gather_scales("xs1", l_offs)
         xs2 = gather_scales("xs2", l_two)
-        xg3 = gather_words("xg3", l_three)
+        xg3 = gather_words("xg3", l_three, "xg3")
         w3 = deal("w3", w3r[:], I32, "w13")
-        ws3 = deal("ws3", ws[:, 2 * N :], U8, "ws13")
+        ws3 = deal("ws3", ws[2][:], U8, "ws13")
         bg = [sb("bg%d" % t, [P, N], F32) for t in range(PACK)]
         nbg = [sb("nbg%d" % t, [P, N], F32) for t in range(PACK)]
         for t in range(PACK):
@@ -146,8 +147,8 @@ def tile_picked_twkpathbwindthree_none_po_kernel(
             nc.scalar.copy(win_b[t][:, :N], acc[:])
             nc.scalar.activation(bg[t][:], acc[:], ACT.Copy, scale=gb_pos[:, t : t + 1])
             nc.scalar.activation(nbg[t][:], acc[:], ACT.Copy, scale=gb_neg[:, t : t + 1])
-        xg1 = gather_words("xg1", l_offs)
-        xg2 = gather_words("xg2", l_two)
+        xg1 = gather_words("xg1", l_offs, "w3r")
+        xg2 = gather_words("xg2", l_two, "ws_raw2")
 
         turned = [bank() for jb in range(4)]
         for t in range(PACK):
@@ -157,9 +158,9 @@ def tile_picked_twkpathbwindthree_none_po_kernel(
             nc.vector.tensor_tensor(minus, win_b[t][:].indirect(l6[:]), nbg[t][:], ALU.mult)
             if t == 0:
                 w1 = deal("w1", w1r[:], I32, "w13")
-                ws1 = deal("ws1", ws[:, :N], U8, "ws13")
+                ws1 = deal("ws1", ws[0][:], U8, "ws13")
                 w2 = deal("w2", w2r[:], I32, "w2")
-                ws2 = deal("ws2", ws[:, N : 2 * N], U8, "ws2")
+                ws2 = deal("ws2", ws[1][:], U8, "ws2")
             nc.scalar.activation(win_a[t][:, :N], project(w1, ws1, xg1, xs1, t)[:], ACT.Copy, scale=ga_abs[:, t : t + 1])
             nc.scalar.activation(win_d[t][:, :N], project(w2, ws2, xg2, xs2, t)[:], ACT.Copy, scale=ga_abs[:, t : t + 1])
             for jb in range(4):
@@ -167,7 +168,7 @@ def tile_picked_twkpathbwindthree_none_po_kernel(
                 dst = turned[jb][:, t * P : (t + 1) * P]
                 nc.tensor.matmul(dst, plus[:, cols], ident[:], start=True, stop=False, is_transpose=True)
                 nc.tensor.matmul(dst, minus[:, cols], ident[:], start=False, stop=True, is_transpose=True)
-        z2b = sb("z2b", [P, N * PACK], BF16)
+        z2b = keep.tile([P, N * PACK], BF16, name="z2b", tag="z2b", align_bytes=64)
         for jh in range(2):
             back = bank()
             for jl in range(2):
@@ -187,7 +188,7 @@ def tile_picked_twkpathbwindthree_none_po_kernel(
         first = sb("first", [P, PACK, N], F32)
         second = sb("second", [P, PACK, N], F32)
         for t in range(PACK):
-            y1 = sb("y1_%d" % t, [P, N], F32)
+            y1 = keep.tile([P, N], F32, name="y1", tag="z2b" if t == 2 else "y1_%d" % t, align_bytes=64)
             y2 = sb("y2_%d" % t, [P, N], F32)
             nc.vector.tensor_copy(y1[:], win_a[t][:].indirect(l1[:]))
             nc.vector.tensor_copy(y2[:], win_a[t][:].indirect(l2[:]))

@@ -140,8 +140,8 @@ def tile_picked_twkpathbwindthree_none_po_kernel(
         xg3 = gather_words("xg3", l_three, "xg3")
         w3 = deal("w3", w3r[:], I32, "w13")
         ws3 = deal("ws3", ws[2][:], U8, "ws13")
-        bg = [sb("bg%d" % t, [P, N], F32) for t in range(PACK)]
-        nbg = [sb("nbg%d" % t, [P, N], F32) for t in range(PACK)]
+        bg = [keep.tile([P, N], F32, name="bg%d" % t, tag="bg%d" % t, align_bytes=64) for t in range(PACK)]
+        nbg = [keep.tile([P, N], F32, name="nbg%d" % t, tag="nbg%d" % t, align_bytes=64) for t in range(PACK)]
         for t in range(PACK):
             acc = project(w3, ws3, xg3, xs3, t)
             nc.scalar.copy(win_b[t][:, :N], acc[:])
@@ -157,12 +157,15 @@ def tile_picked_twkpathbwindthree_none_po_kernel(
             nc.vector.tensor_tensor(plus, win_b[t][:].indirect(l5[:]), bg[t][:], ALU.mult)
             nc.vector.tensor_tensor(minus, win_b[t][:].indirect(l6[:]), nbg[t][:], ALU.mult)
             if t == 0:
-                w1 = deal("w1", w1r[:], I32, "w13")
-                ws1 = deal("ws1", ws[0][:], U8, "ws13")
-                w2 = deal("w2", w2r[:], I32, "w2")
-                ws2 = deal("ws2", ws[1][:], U8, "ws2")
-            nc.scalar.activation(win_a[t][:, :N], project(w1, ws1, xg1, xs1, t)[:], ACT.Copy, scale=ga_abs[:, t : t + 1])
-            nc.scalar.activation(win_d[t][:, :N], project(w2, ws2, xg2, xs2, t)[:], ACT.Copy, scale=ga_abs[:, t : t + 1])
+                w1 = deal("w1", w1r[:], I32, "bg0")
+                ws1 = deal("ws1", ws[0][:], U8, "nbg0")
+                for f in range(PACK):
+                    nc.scalar.activation(win_a[f][:, :N], project(w1, ws1, xg1, xs1, f)[:], ACT.Copy, scale=ga_abs[:, f : f + 1])
+            if t == 1:
+                w2 = deal("w2", w2r[:], I32, "bg1")
+                ws2 = deal("ws2", ws[1][:], U8, "nbg1")
+                for f in range(PACK):
+                    nc.scalar.activation(win_d[f][:, :N], project(w2, ws2, xg2, xs2, f)[:], ACT.Copy, scale=ga_abs[:, f : f + 1])
             for jb in range(4):
                 cols = slice(jb * P, (jb + 1) * P)
                 dst = turned[jb][:, t * P : (t + 1) * P]

from contextlib import ExitStack

import concourse.mybir as mybir
from concourse.masks import make_identity

F32 = mybir.dt.float32
BF16 = mybir.dt.bfloat16
I32 = mybir.dt.int32
U32 = mybir.dt.uint32
U16 = mybir.dt.uint16
U8 = mybir.dt.uint8
FP8X4 = mybir.dt.float8_e4m3fn_x4
ALU = mybir.AluOpType
ACT = mybir.ActivationFunctionType

P = 128
PACK = 4
T = 2048
N = 512
HALF = N // 2
OUT_SLICES = ((0, 256), (256, 384), (384, 512))
FLOPS = 4 * 2 * 512 * 512 * 512


def tile_picked_twkpathbwindthree_none_po_kernel(
    tc, x_words, x_scales, w1_words, w1_scales, w2_words, w2_scales, w3_words, w3_scales, ga, gb,
    offs, two, n1, n2, n3, n4, three, n5, n6, n7, n8, n9, out_0, out_1, out_2,
):
    nc = tc.nc
    with ExitStack() as ctx:
        lists = ctx.enter_context(tc.tile_pool(name="lists", bufs=1))
        keep = ctx.enter_context(tc.tile_pool(name="keep", bufs=1))
        psum = ctx.enter_context(tc.psum_pool(name="psum", bufs=8))

        def sb(name, shape, dtype):
            return keep.tile(shape, dtype, name=name, align_bytes=64)

        def bank():
            return psum.tile([P, N], F32, name="bank")

        def load_list(name, dram):
            tile = lists.tile([P, N // 16], U16, name=name)
            nc.sync.dma_start(tile[:], dram)
            return tile

        def load_scales(plane, dram):
            for q in range(4):
                nc.sync.dma_start(plane[32 * q : 32 * q + 4, :].bitcast(I32), dram[0][4 * q : 4 * q + 4, :].bitcast(I32))

        def load_words(name, dram, width):
            tile = keep.tile([P, width], I32, name=name, tag=name, align_bytes=64)
            nc.sync.dma_start(tile[:], dram[0].rearrange("p n t -> p (n t)").bitcast(I32))
            return tile

        def load_gain(rows, dram):
            nc.sync.dma_start(rows.rearrange("t (g r) -> t g r", r=8), dram.rearrange("(g t r) o -> t g (r o)", t=PACK, r=8))

        def entries(tile, lo, hi):
            return tile[:, lo // 16 : hi // 16]

        xs = sb("xs", [P, T], U8)
        ws = [keep.tile([P, N], U8, name="ws_raw%d" % i, tag="ws_raw%d" % i, align_bytes=64) for i in range(3)]
        gain_rows = sb("gain_rows", [P, P], F32)
        nc.vector.memset(xs[:].bitcast(I32), 0)
        nc.vector.memset(gain_rows[:], 0.0)
        for plane in reversed(ws):
            nc.vector.memset(plane[:].bitcast(I32), 0)
        win_a = [sb("win_a%d" % t, [P, 2 * N], F32) for t in range(PACK)]
        win_d = [sb("win_d%d" % t, [P, 2 * N], F32) for t in range(PACK)]
        win_b = [sb("win_b%d" % t, [P, 2 * N], F32) for t in range(PACK)]
        for t in range(PACK):
            nc.vector.memset(win_b[t][:, N:], 0.0)

        l_three = load_list("l_three", three)
        l_offs = load_list("l_offs", offs)
        l_two = load_list("l_two", two)
        load_scales(xs[:], x_scales)
        xw = load_words("xw", x_words, T)
        load_gain(gain_rows[0:PACK, :], ga)
        load_gain(gain_rows[PACK : 2 * PACK, :], gb)
        load_scales(ws[2][:], w3_scales)
        w3r = load_words("w3r", w3_words, N)
        l5 = load_list("l5", n5)
        l6 = load_list("l6", n6)
        load_scales(ws[0][:], w1_scales)
        load_scales(ws[1][:], w2_scales)
        w1r = load_words("w1r", w1_words, N)
        w2r = load_words("w2r", w2_words, N)
        l1 = load_list("l1", n1)
        l3 = load_list("l3", n3)
        l2 = load_list("l2", n2)
        l4 = load_list("l4", n4)
        l7 = load_list("l7", n7)
        l8 = load_list("l8", n8)
        l9 = load_list("l9", n9)

        ident = sb("ident", [P, P], F32)
        make_identity(nc, ident[:])

        ga_abs = sb("ga_abs", [P, PACK], F32)
        ga_negsign = sb("ga_negsign", [P, PACK], F32)
        gb_neg = sb("gb_neg", [P, PACK], F32)
        gains = bank()
        nc.tensor.transpose(gains[:, :P], gain_rows[:], ident[:])
        nc.scalar.activation(ga_abs[:], gains[:, 0:PACK], ACT.Abs)
        nc.scalar.activation(ga_negsign[:], gains[:, 0:PACK], ACT.Sign, scale=-1.0)
        for t in range(PACK):
            nc.scalar.activation(gb_neg[:, t : t + 1], gains[:, PACK + t : PACK + t + 1], ACT.Copy, scale=ga_negsign[:, t : t + 1])
        gb_pos = sb("gb_pos", [P, PACK], F32)
        nc.scalar.activation(gb_pos[:], gb_neg[:], ACT.Copy, scale=-1.0)

        def gather_scales(name, lst):
            tile = sb(name, [P, N], U8)
            nc.vector.tensor_copy(tile[:], xs[:].indirect(lst[:]))
            return tile

        def gather_words(name, lst, tag):
            tile = keep.tile([P, N], U32, name=name, tag=tag, align_bytes=64)
            nc.vector.tensor_copy(tile[:], xw[:].bitcast(U32).indirect(lst[:]))
            return tile

        def deal(name, raw, dtype, tag):
            tile = keep.tile([P, N], dtype, name=name, tag=tag, align_bytes=64)
            nc.vector.tensor_copy(
                tile[:].bitcast(I32).rearrange("p (t g r) -> p g t r", t=PACK, g=16),
                raw.bitcast(I32).rearrange("p (g t r) -> p g t r", t=PACK, g=16),
            )
            return tile

        def project(w, wscale, xg, xsg, t):
            acc = bank()
            cols = slice(t * P, (t + 1) * P)
            nc.tensor.matmul_mx(acc[:], lhsT=w[:, cols].bitcast(FP8X4), lhsT_scale=wscale[:, cols],
                                rhs=xg[:].bitcast(FP8X4), rhs_scale=xsg[:], start=True, stop=True)
            return acc

        xs3 = gather_scales("xs3", l_three)
        xs1 = gather_scales("xs1", l_offs)
        xs2 = gather_scales("xs2", l_two)
        xg3 = gather_words("xg3", l_three, "xg3")
        w3 = deal("w3", w3r[:], I32, "w13")
        ws3 = deal("ws3", ws[2][:], U8, "ws13")
        bg = [keep.tile([P, N], F32, name="bg%d" % t, tag="bg%d" % t, align_bytes=64) for t in range(PACK)]
        nbg = [keep.tile([P, N], F32, name="nbg%d" % t, tag="nbg%d" % t, align_bytes=64) for t in range(PACK)]
        for t in range(PACK):
            acc = project(w3, ws3, xg3, xs3, t)
            nc.scalar.copy(win_b[t][:, :N], acc[:])
            nc.scalar.activation(bg[t][:], acc[:], ACT.Copy, scale=gb_pos[:, t : t + 1])
            nc.scalar.activation(nbg[t][:], acc[:], ACT.Copy, scale=gb_neg[:, t : t + 1])
        xg1 = gather_words("xg1", l_offs, "w3r")
        xg2 = gather_words("xg2", l_two, "ws_raw2")

        turned = [bank() for jb in range(4)]
        for t in range(PACK):
            plus = win_a[t][:, N:]
            minus = win_d[t][:, N:]
            nc.vector.tensor_tensor(plus, win_b[t][:].indirect(l5[:]), bg[t][:], ALU.mult)
            nc.vector.tensor_tensor(minus, win_b[t][:].indirect(l6[:]), nbg[t][:], ALU.mult)
            if t == 0:
                w1 = deal("w1", w1r[:], I32, "bg0")
                ws1 = deal("ws1", ws[0][:], U8, "nbg0")
                for f in range(PACK):
                    nc.scalar.activation(win_a[f][:, :N], project(w1, ws1, xg1, xs1, f)[:], ACT.Copy, scale=ga_abs[:, f : f + 1])
            if t == 1:
                w2 = deal("w2", w2r[:], I32, "bg1")
                ws2 = deal("ws2", ws[1][:], U8, "nbg1")
                for f in range(PACK):
                    nc.scalar.activation(win_d[f][:, :N], project(w2, ws2, xg2, xs2, f)[:], ACT.Copy, scale=ga_abs[:, f : f + 1])
            for jb in range(4):
                cols = slice(jb * P, (jb + 1) * P)
                dst = turned[jb][:, t * P : (t + 1) * P]
                nc.tensor.matmul(dst, plus[:, cols], ident[:], start=True, stop=False, is_transpose=True)
                nc.tensor.matmul(dst, minus[:, cols], ident[:], start=False, stop=True, is_transpose=True)
        z2b = keep.tile([P, N * PACK], BF16, name="z2b", tag="z2b", align_bytes=64)
        for jh in range(2):
            back = bank()
            for jl in range(2):
                jb = 2 * jh + jl
                rows = sb("z2_rows%d" % jb, [P, N], BF16)
                nc.scalar.copy(rows[:].rearrange("c (u p e) -> c u p e", u=2, e=2), turned[jb][:].rearrange("c (u e p) -> c u p e", u=2, e=2))
                for u in range(2):
                    nc.tensor.transpose(back[:, u * HALF + jl * P : u * HALF + (jl + 1) * P], rows[:].bitcast(F32)[:, u * P : (u + 1) * P], ident[:])
            nc.scalar.copy(
                z2b[:].bitcast(F32)[:, jh * N : (jh + 1) * N].rearrange("p (v u) -> p v u", u=2),
                back[:].rearrange("p (u v) -> p v u", u=2),
            )
        z2q = sb("z2q", [P, N], U32)
        z2s = sb("z2s", [P, N], U8)
        nc.vector.quantize_mx(z2q[:].bitcast(FP8X4), z2s[:], z2b[:])

        first = sb("first", [P, PACK, N], F32)
        second = sb("second", [P, PACK, N], F32)
        for t in range(PACK):
            y1 = keep.tile([P, N], F32, name="y1", tag="z2b" if t == 2 else "y1_%d" % t, align_bytes=64)
            y2 = sb("y2_%d" % t, [P, N], F32)
            nc.vector.tensor_copy(y1[:], win_a[t][:].indirect(l1[:]))
            nc.vector.tensor_copy(y2[:], win_a[t][:].indirect(l2[:]))
            nc.vector.tensor_tensor(first[:, t, :], win_d[t][:].indirect(l3[:]), y1[:], ALU.add)
            nc.vector.tensor_tensor(second[:, t, :], win_d[t][:].indirect(l4[:]), y2[:], ALU.add)
        zq = sb("zq", [P, N], U32)
        zs = sb("zs", [P, N], U8)
        s_plain = [sb("s_plain%d" % r, [P, N], F32) for r in range(PACK)]
        for h in range(2):
            zb = sb("zb", [P, HALF * PACK], BF16)
            nc.vector.tensor_tensor(
                zb[:].rearrange("p (r m t) -> p m t r", r=2, t=PACK),
                first[:].rearrange("p t (m r) -> p m t r", r=PACK)[:, :, :, 2 * h : 2 * h + 2],
                second[:].rearrange("p t (m r) -> p m t r", r=PACK)[:, :, :, 2 * h : 2 * h + 2],
                ALU.max,
            )
            cols = slice(h * HALF, (h + 1) * HALF)
            nc.vector.quantize_mx(zq[:, cols].bitcast(FP8X4), zs[:, cols], zb[:])
        for r in range(PACK):
            cols = slice(r * P, (r + 1) * P)
            acc = bank()
            nc.tensor.matmul_mx(acc[:], lhsT=zq[:, cols].bitcast(FP8X4), lhsT_scale=zs[:, cols],
                                rhs=z2q[:].bitcast(FP8X4), rhs_scale=z2s[:], start=True, stop=True)
            nc.scalar.activation(win_a[r][:, :N], acc[:], ACT.Copy, scale=-0.0625)
            nc.scalar.activation(s_plain[r][:], acc[:], ACT.Copy, scale=0.0625)

        at8 = [sb("at8_%d" % r, [P, N], F32) for r in range(PACK)]
        su = [sb("su%d" % r, [P, N], F32) for r in range(PACK)]
        half_su = [sb("half_su%d" % r, [P, N], F32) for r in range(PACK)]
        for r in range(PACK):
            nc.vector.tensor_tensor(win_d[r][:, :N], win_a[r][:].indirect(l7[:]), s_plain[r][:], ALU.add)
        for r in range(PACK + 1):
            if r < PACK:
                nc.vector.tensor_copy(at8[r][:], win_d[r][:].indirect(l8[:]))
            if r > 0:
                nc.vector.tensor_tensor(su[r - 1][:], win_d[r - 1][:, :N], at8[r - 1][:], ALU.max)
                nc.scalar.activation(half_su[r - 1][:], su[r - 1][:], ACT.Copy, scale=0.5)
        out_rows = out_0.rearrange("(p r) v -> p r v", r=PACK)
        out_words = out_1[0].rearrange("p c r -> p (c r)").bitcast(I32)
        os_ = sb("os", [P, N], U8)
        for i, (lo, hi) in enumerate(OUT_SLICES):
            width = hi - lo
            res = sb("res%d" % i, [P, PACK, width], F32)
            for r in range(PACK):
                nc.vector.tensor_tensor(res[:, r, :], half_su[r][:].indirect(entries(l9, lo, hi)), su[r][:, lo:hi], ALU.add)
            nc.sync.dma_start(out_rows[:, :, lo:hi], res[:])
            ob = sb("ob%d" % i, [P, width * PACK], BF16)
            weave_out = ob[:].rearrange("p (c i r) -> p c r i", i=4, r=PACK)
            weave_in = res[:].rearrange("p r (c i) -> p c r i", i=4)
            if hi < N:
                nc.scalar.copy(weave_out, weave_in)
            else:
                nc.vector.tensor_copy(weave_out, weave_in)
            oq = sb("oq%d" % i, [P, width], I32)
            nc.vector.quantize_mx(oq[:].bitcast(FP8X4), os_[:, lo:hi], ob[:])
            nc.scalar.dma_start(out_words[:, lo:hi], oq[:])
        for q in range(4):
            queue = nc.sync if q % 2 == 0 else nc.scalar
            queue.dma_start(out_2[0][4 * q : 4 * q + 4, :].bitcast(I32), os_[32 * q : 32 * q + 4, :].bitcast(I32))
